import numpy as np
import ml_dtypes


def mxq(x, axis, fmt="e4m3"):
    dtype, down = {"e4m3": (ml_dtypes.float8_e4m3fn, 7), "e5m2": (ml_dtypes.float8_e5m2, 14)}[fmt]
    v = np.moveaxis(np.asarray(x, np.float32).astype(ml_dtypes.bfloat16).astype(np.float64), axis, -1)
    blocks = v.reshape(v.shape[:-1] + (-1, 32))
    amax = np.abs(blocks).max(-1, keepdims=True)
    byte = np.maximum(np.where(amax > 0, np.frexp(amax)[1] - 1 + 127, 0) - down, 1)
    scale = np.exp2(byte - 127.0)
    codes = (blocks / scale).astype(np.float32).astype(dtype).astype(np.float64)
    return np.moveaxis((codes * scale).reshape(v.shape), -1, axis)


WIDE = False


def mx_kscale(k, group=512):
    if not WIDE:
        return np.ones(k)
    levels = np.array([10, -10, 5, -5, 0])
    if group != 512:
        return np.exp2(np.random.permutation(np.resize(levels, k // group))).repeat(group)
    if k % 512:
        return np.exp2(np.random.permutation(np.resize(levels, k // 32))).repeat(32)
    a = np.empty((k // 512, 16))
    for p in range(k // 512):
        a[p, :8] = np.random.permutation(np.resize(levels, 8))
        for g in range(8):
            far = levels[np.abs(levels - a[p, g]) >= 10]
            a[p, g + 8] = far[np.random.randint(len(far))]
    return np.exp2(a.ravel()).repeat(32)


def f64(x):
    return np.asarray(x).astype(np.float64)


E2M1 = np.array([0.0, 0.5, 1.0, 1.5, 2.0, 3.0, 4.0, 6.0, -0.0, -0.5, -1.0, -1.5, -2.0, -3.0, -4.0, -6.0])


def pack_group(w):
    k, n = w.shape
    w = f64(np.asarray(w, np.float32).astype(ml_dtypes.bfloat16)).reshape(k // 32, 32, n)
    amax = np.abs(w).max(1)
    mant, ex = np.frexp(amax / 6.0)
    byte = np.clip(np.where(amax > 0, np.where(mant > 0.5, ex, ex - 1) + 127, 1), 1, 254)
    scaled = (w * np.exp2(127.0 - byte)[:, None, :]).reshape(k, n).astype(np.float32)
    c = np.ascontiguousarray(scaled.reshape(k // 4, 4, n).transpose(0, 2, 1)).astype(ml_dtypes.float4_e2m1fn).view(np.uint8) & 0xF
    return np.ascontiguousarray((c[..., 0::2] | (c[..., 1::2] << 4)).reshape(k // 4, 2 * n)), byte.astype(np.uint8)


def unpack_group(words, scales):
    p, n = words.shape[0], scales.shape[1]
    words = np.ascontiguousarray(words).reshape(p, n, 2)
    nib = np.empty((p, n, 4), np.uint8)
    nib[..., 0::2] = words & 0xF
    nib[..., 1::2] = words >> 4
    return E2M1[nib].transpose(0, 2, 1).reshape(4 * p, n) * np.repeat(np.exp2(scales.astype(np.float64) - 127.0), 32, axis=0)


G, D, M, O, N = 2, 256, 256, 256, 512


def setup_inputs():
    n = np.random.standard_normal
    s_d = mx_kscale(D, 0)
    s_o = mx_kscale(O, 0)
    w1_ = [pack_group(w) for w in n((G, D, M)) / np.sqrt(D) / s_d[:, None]]
    w2_ = [pack_group(w) for w in n((G, D, M)) / np.sqrt(D) / s_d[:, None]]
    wo_ = [pack_group(w) for w in n((G, O, M)) / np.sqrt(O) / s_o[:, None]]
    return {
        "x": (n((G, D, N)) * s_d[:, None]).astype(np.float32),
        "w1_words": np.stack([w[0] for w in w1_]),
        "w1_scales": np.stack([w[1] for w in w1_]),
        "w2_words": np.stack([w[0] for w in w2_]),
        "w2_scales": np.stack([w[1] for w in w2_]),
        "tp": (np.random.uniform(0.6, 2.0, (G, M, 1))).astype(np.float32),
        "wo_words": np.stack([w[0] for w in wo_]),
        "wo_scales": np.stack([w[1] for w in wo_]),
        "dy": (n((G, O, N)) * s_o[:, None]).astype(np.float32),
        "old": (0.3 * n((G, M, N))).astype(np.float32),
    }


def reference(x, w1_words, w1_scales, w2_words, w2_scales, tp, wo_words, wo_scales, dy, old):
    w1 = np.stack([unpack_group(w1_words[g], w1_scales[g]) for g in range(G)])
    xq = mxq(f64(x), 1, "e4m3")
    z1 = w1.transpose(0, 2, 1) @ xq
    w2 = np.stack([unpack_group(w2_words[g], w2_scales[g]) for g in range(G)])
    z2 = w2.transpose(0, 2, 1) @ xq
    se = np.exp(z1 * f64(tp)) + np.exp(z2 * f64(tp))
    wo = np.stack([unpack_group(wo_words[g], wo_scales[g]) for g in range(G)])
    dyq = mxq(f64(dy), 1, "e4m3")
    c0 = wo.transpose(0, 2, 1) @ dyq
    dse = c0 / f64(tp) / se
    dz1 = dse * np.exp(z1 * f64(tp)) * f64(tp)
    y = dz1 + f64(old)
    return y

@@ -1,0 +1,169 @@
+from contextlib import ExitStack
+
+import concourse.mybir as mybir
+
+G, D, M, N = 2, 256, 256, 512
+FLOPS = 3 * 2 * G * D * M * N
+
+F32 = mybir.dt.float32
+BF16 = mybir.dt.bfloat16
+I32 = mybir.dt.int32
+U32 = mybir.dt.uint32
+U8 = mybir.dt.uint8
+FP8X4 = mybir.dt.float8_e4m3fn_x4
+FP4X4 = mybir.dt.float4_e2m1fn_x4
+ALU = mybir.AluOpType
+ACT = mybir.ActivationFunctionType
+
+P = 128
+PACK = 4
+ROWS = D // PACK
+HALVES = M // P
+TILES = [(g, h) for h in range(HALVES) for g in range(G)]
+X_SPLIT = 336
+DY_SPLIT = 384
+
+
+def load_words(queue, tile, words):
+    queue.dma_start(out=tile[:].bitcast(I32), in_=words.rearrange("g p b -> (g p) b").bitcast(I32))
+
+
+def load_scales(queue, tile, scales):
+    rows = scales.rearrange("g t m -> (g t) m").bitcast(I32)
+    for q in range(4):
+        queue.dma_start(out=tile[32 * q : 32 * q + 4, :].bitcast(I32), in_=rows[4 * q : 4 * q + 4, :])
+
+
+def interleave(copy, packed, raw, n0, n1):
+    copy(
+        out=packed[:, n0:n1, :].rearrange("p (c i) j -> p c j i", i=4),
+        in_=raw[:, :, n0:n1].rearrange("p j (c i) -> p c j i", i=4),
+    )
+
+
+def tile_rows_bsoftmaxoftwo_kernel(
+    tc, x, w1_words, w1_scales, w2_words, w2_scales, tp, wo_words, wo_scales, dy, old, out
+):
+    nc = tc.nc
+    with ExitStack() as ctx:
+        sb = ctx.enter_context(tc.tile_pool(name="sb", bufs=1))
+        psum = ctx.enter_context(tc.psum_pool(name="psum", bufs=1))
+        ctx.enter_context(tc.manual_schedule())
+
+        x_raw = sb.tile([P, PACK, N], F32, name="x_raw")
+        dy_raw = sb.tile([P, PACK, N], F32, name="dy_raw")
+        x_packed = sb.tile([P, N, PACK], BF16, name="x_packed", align_bytes=64)
+        dy_packed = sb.tile([P, N, PACK], BF16, name="dy_packed", align_bytes=64)
+        x_codes = sb.tile([P, N], U32, name="x_codes", align_bytes=64)
+        dy_codes = sb.tile([P, N], U32, name="dy_codes", align_bytes=64)
+        x_scales = sb.tile([P, N], U8, name="x_scales", align_bytes=64)
+        dy_scales = sb.tile([P, N], U8, name="dy_scales", align_bytes=64)
+        w1 = sb.tile([P, 2 * M], U8, name="w1", align_bytes=64)
+        w2 = sb.tile([P, 2 * M], U8, name="w2", align_bytes=64)
+        wo = sb.tile([P, 2 * M], U8, name="wo", align_bytes=64)
+        s1 = sb.tile([P, M], U8, name="s1", align_bytes=64)
+        s2 = sb.tile([P, M], U8, name="s2", align_bytes=64)
+        so = sb.tile([P, M], U8, name="so", align_bytes=64)
+        temper = sb.tile([P, G, HALVES], F32, name="temper")
+        warm_in = sb.tile([P, 1], F32, name="warm_in")
+        warm_out = sb.tile([P, 1], F32, name="warm_out")
+        old_sb = [sb.tile([P, G, N], F32, name="old%d" % h) for h in range(HALVES)]
+        z2_sb = [sb.tile([P, N], F32, name="z2_sb%d" % t) for t in range(4)]
+        diff = [sb.tile([P, N], F32, name="diff%d" % t) for t in range(4)]
+        share = [sb.tile([P, N], F32, name="share%d" % t) for t in range(4)]
+        grad = [sb.tile([P, N], F32, name="grad%d" % t) for t in range(4)]
+        result = [sb.tile([P, N], F32, name="result%d" % t) for t in range(4)]
+        bank_a = [psum.tile([P, N], F32, name="bank_a%d" % t) for t in range(4)]
+        bank_b = [psum.tile([P, N], F32, name="bank_b%d" % t) for t in range(4)]
+
+        def product(bank, words, wscales, codes, scales, t):
+            g, h = TILES[t]
+            rows = slice(ROWS * g, ROWS * (g + 1))
+            nc.tensor.matmul_mx(
+                out=bank[:],
+                lhsT=words[rows, 2 * P * h : 2 * P * (h + 1)].bitcast(FP4X4),
+                lhsT_scale=wscales[rows, P * h : P * (h + 1)],
+                rhs=codes[rows, :].bitcast(FP8X4),
+                rhs_scale=scales[rows, :],
+                start=True,
+                stop=True,
+            )
+
+        def quantize(codes, scales, packed):
+            nc.vector.quantize_mx(
+                out=codes[:].bitcast(FP8X4), scales=scales[:], in_=packed[:].rearrange("p n j -> p (n j)")
+            )
+
+        def copy_z2(t):
+            nc.scalar.copy(out=z2_sb[t][:], in_=bank_a[t][:])
+
+        def subtract(t):
+            nc.vector.tensor_tensor(out=diff[t][:], in0=bank_b[t][:], in1=z2_sb[t][:], op=ALU.subtract)
+
+        def sigmoid(t):
+            g, h = TILES[t]
+            nc.scalar.activation(out=share[t][:], in_=diff[t][:], func=ACT.Sigmoid, scale=temper[:, g, h : h + 1])
+
+        def multiply(t):
+            nc.vector.tensor_tensor(out=grad[t][:], in0=bank_a[t][:], in1=share[t][:], op=ALU.mult)
+
+        def add_old(engine, t, n0=0, n1=N):
+            g, h = TILES[t]
+            engine.tensor_tensor(out=result[t][:, n0:n1], in0=grad[t][:, n0:n1], in1=old_sb[h][:, g, n0:n1], op=ALU.add)
+
+        def store(t, queue=nc.sync):
+            g, h = TILES[t]
+            queue.dma_start(out=out[g, P * h : P * (h + 1), :], in_=result[t][:])
+
+        for plane in (s2, s1, so):
+            nc.vector.memset(plane[:].bitcast(I32), 0)
+        nc.vector.memset(warm_in[:], 0.0)
+        nc.scalar.activation(out=warm_out[:], in_=warm_in[:], func=ACT.Sigmoid)
+
+        nc.sync.dma_start(out=x_raw[:], in_=x.rearrange("g (p j) n -> (g p) j n", j=PACK))
+        load_words(nc.sync, w2, w2_words)
+        load_words(nc.sync, w1, w1_words)
+        load_scales(nc.sync, s1, w1_scales)
+        nc.sync.dma_start(out=dy_raw[:], in_=dy.rearrange("g (p j) n -> (g p) j n", j=PACK))
+        load_scales(nc.gpsimd, s2, w2_scales)
+        with nc.allow_non_contiguous_dma(reason="one temper a partition"):
+            nc.gpsimd.dma_start(out=temper[:], in_=tp.rearrange("g (h p) o -> p g (h o)", p=P))
+        load_words(nc.sync, wo, wo_words)
+        load_scales(nc.sync, so, wo_scales)
+        for h in range(HALVES):
+            nc.sync.dma_start(out=old_sb[h][:], in_=old[:, P * h : P * (h + 1), :].rearrange("g p n -> p g n"))
+
+        interleave(nc.vector.tensor_copy, x_packed, x_raw, 0, X_SPLIT)
+        interleave(nc.scalar.copy, x_packed, x_raw, X_SPLIT, N)
+        quantize(x_codes, x_scales, x_packed)
+        for h in range(HALVES):
+            for t in (2 * h, 2 * h + 1):
+                product(bank_a[t], w2, s2, x_codes, x_scales, t)
+            for t in (2 * h, 2 * h + 1):
+                product(bank_b[t], w1, s1, x_codes, x_scales, t)
+
+        copy_z2(0)
+        interleave(nc.vector.tensor_copy, dy_packed, dy_raw, 0, DY_SPLIT)
+        interleave(nc.scalar.copy, dy_packed, dy_raw, DY_SPLIT, N)
+        copy_z2(1)
+        subtract(0)
+        quantize(dy_codes, dy_scales, dy_packed)
+        copy_z2(2)
+        subtract(1)
+        copy_z2(3)
+        for t in range(4):
+            product(bank_a[t], wo, so, dy_codes, dy_scales, t)
+        sigmoid(0)
+        subtract(2)
+        sigmoid(1)
+        subtract(3)
+        sigmoid(2)
+        sigmoid(3)
+        for t in range(4):
+            multiply(t)
+            if t < 2:
+                add_old(nc.gpsimd, t)
+                store(t)
+        for t in (2, 3):
+            add_old(nc.vector, t)
+            store(t)

@@ -21,16 +21,16 @@ ROWS = D // PACK
 HALVES = M // P
 TILES = [(g, h) for h in range(HALVES) for g in range(G)]
 X_SPLIT = 336
-DY_SPLIT = 384
+DY_SPLIT = 368
 
 
 def load_words(queue, tile, words):
     queue.dma_start(out=tile[:].bitcast(I32), in_=words.rearrange("g p b -> (g p) b").bitcast(I32))
 
 
-def load_scales(queue, tile, scales):
+def load_scales(queue, tile, scales, quadrants=(0, 1, 2, 3)):
     rows = scales.rearrange("g t m -> (g t) m").bitcast(I32)
-    for q in range(4):
+    for q in quadrants:
         queue.dma_start(out=tile[32 * q : 32 * q + 4, :].bitcast(I32), in_=rows[4 * q : 4 * q + 4, :])
 
 
@@ -73,8 +73,10 @@ def tile_rows_bsoftmaxoftwo_kernel(
         share = [sb.tile([P, N], F32, name="share%d" % t) for t in range(4)]
         grad = [sb.tile([P, N], F32, name="grad%d" % t) for t in range(4)]
         result = [sb.tile([P, N], F32, name="result%d" % t) for t in range(4)]
-        bank_a = [psum.tile([P, N], F32, name="bank_a%d" % t) for t in range(4)]
-        bank_b = [psum.tile([P, N], F32, name="bank_b%d" % t) for t in range(4)]
+        banks = [[psum.tile([P, N], F32, name="bank%d_%d" % (g, i)) for i in range(4)] for g in range(G)]
+        z2_bank = [banks[g][2 * h] for g, h in TILES]
+        z1_bank = [banks[g][1 - h] for g, h in TILES]
+        c0_bank = [banks[g][3 - 2 * h] for g, h in TILES]
 
         def product(bank, words, wscales, codes, scales, t):
             g, h = TILES[t]
@@ -95,17 +97,17 @@ def tile_rows_bsoftmaxoftwo_kernel(
             )
 
         def copy_z2(t):
-            nc.scalar.copy(out=z2_sb[t][:], in_=bank_a[t][:])
+            nc.scalar.copy(out=z2_sb[t][:], in_=z2_bank[t][:])
 
         def subtract(t):
-            nc.vector.tensor_tensor(out=diff[t][:], in0=bank_b[t][:], in1=z2_sb[t][:], op=ALU.subtract)
+            nc.vector.tensor_tensor(out=diff[t][:], in0=z1_bank[t][:], in1=z2_sb[t][:], op=ALU.subtract)
 
         def sigmoid(t):
             g, h = TILES[t]
             nc.scalar.activation(out=share[t][:], in_=diff[t][:], func=ACT.Sigmoid, scale=temper[:, g, h : h + 1])
 
         def multiply(t):
-            nc.vector.tensor_tensor(out=grad[t][:], in0=bank_a[t][:], in1=share[t][:], op=ALU.mult)
+            nc.vector.tensor_tensor(out=grad[t][:], in0=c0_bank[t][:], in1=share[t][:], op=ALU.mult)
 
         def add_old(engine, t, n0=0, n1=N):
             g, h = TILES[t]
@@ -120,12 +122,13 @@ def tile_rows_bsoftmaxoftwo_kernel(
         nc.vector.memset(warm_in[:], 0.0)
         nc.scalar.activation(out=warm_out[:], in_=warm_in[:], func=ACT.Sigmoid)
 
-        nc.sync.dma_start(out=x_raw[:], in_=x.rearrange("g (p j) n -> (g p) j n", j=PACK))
         load_words(nc.sync, w2, w2_words)
         load_words(nc.sync, w1, w1_words)
-        load_scales(nc.sync, s1, w1_scales)
+        nc.sync.dma_start(out=x_raw[:], in_=x.rearrange("g (p j) n -> (g p) j n", j=PACK))
+        load_scales(nc.sync, s2, w2_scales)
+        load_scales(nc.sync, s1, w1_scales, (0, 1))
+        load_scales(nc.gpsimd, s1, w1_scales, (2, 3))
         nc.sync.dma_start(out=dy_raw[:], in_=dy.rearrange("g (p j) n -> (g p) j n", j=PACK))
-        load_scales(nc.gpsimd, s2, w2_scales)
         with nc.allow_non_contiguous_dma(reason="one temper a partition"):
             nc.gpsimd.dma_start(out=temper[:], in_=tp.rearrange("g (h p) o -> p g (h o)", p=P))
         load_words(nc.sync, wo, wo_words)
@@ -133,14 +136,24 @@ def tile_rows_bsoftmaxoftwo_kernel(
         for h in range(HALVES):
             nc.sync.dma_start(out=old_sb[h][:], in_=old[:, P * h : P * (h + 1), :].rearrange("g p n -> p g n"))
 
+        def z1_product(t):
+            product(z1_bank[t], w1, s1, x_codes, x_scales, t)
+
+        def z2_product(t):
+            product(z2_bank[t], w2, s2, x_codes, x_scales, t)
+
+        def c0_product(t):
+            product(c0_bank[t], wo, so, dy_codes, dy_scales, t)
+
         interleave(nc.vector.tensor_copy, x_packed, x_raw, 0, X_SPLIT)
         interleave(nc.scalar.copy, x_packed, x_raw, X_SPLIT, N)
         quantize(x_codes, x_scales, x_packed)
-        for h in range(HALVES):
-            for t in (2 * h, 2 * h + 1):
-                product(bank_a[t], w2, s2, x_codes, x_scales, t)
-            for t in (2 * h, 2 * h + 1):
-                product(bank_b[t], w1, s1, x_codes, x_scales, t)
+        z2_product(0)
+        z2_product(1)
+        z1_product(0)
+        z1_product(1)
+        z2_product(2)
+        z2_product(3)
 
         copy_z2(0)
         interleave(nc.vector.tensor_copy, dy_packed, dy_raw, 0, DY_SPLIT)
@@ -148,22 +161,28 @@ def tile_rows_bsoftmaxoftwo_kernel(
         copy_z2(1)
         subtract(0)
         quantize(dy_codes, dy_scales, dy_packed)
-        copy_z2(2)
         subtract(1)
-        copy_z2(3)
-        for t in range(4):
-            product(bank_a[t], wo, so, dy_codes, dy_scales, t)
+        c0_product(0)
+        c0_product(1)
+        z1_product(2)
+        z1_product(3)
+        c0_product(2)
+        c0_product(3)
         sigmoid(0)
-        subtract(2)
+        copy_z2(2)
         sigmoid(1)
-        subtract(3)
-        sigmoid(2)
-        sigmoid(3)
-        for t in range(4):
+        copy_z2(3)
+        for t in (0, 1):
             multiply(t)
-            if t < 2:
-                add_old(nc.gpsimd, t)
-                store(t)
-        for t in (2, 3):
-            add_old(nc.vector, t)
+            add_old(nc.gpsimd, t)
             store(t)
+        for t in (2, 3):
+            subtract(t)
+            sigmoid(t)
+        multiply(2)
+        add_old(nc.gpsimd, 2, 0, N // 2)
+        multiply(3)
+        add_old(nc.vector, 2, N // 2, N)
+        store(2)
+        add_old(nc.vector, 3)
+        store(3, nc.scalar)

@@ -20,8 +20,7 @@ PACK = 4
 ROWS = D // PACK
 HALVES = M // P
 TILES = [(g, h) for h in range(HALVES) for g in range(G)]
-X_SPLIT = 336
-DY_SPLIT = 368
+HALF = N // 2
 
 
 def load_words(queue, tile, words):
@@ -50,10 +49,10 @@ def tile_rows_bsoftmaxoftwo_kernel(
         psum = ctx.enter_context(tc.psum_pool(name="psum", bufs=1))
         ctx.enter_context(tc.manual_schedule())
 
-        x_raw = sb.tile([P, PACK, N], F32, name="x_raw")
-        dy_raw = sb.tile([P, PACK, N], F32, name="dy_raw")
-        x_packed = sb.tile([P, N, PACK], BF16, name="x_packed", align_bytes=64)
-        dy_packed = sb.tile([P, N, PACK], BF16, name="dy_packed", align_bytes=64)
+        x_raw = [sb.tile([P, PACK, HALF], F32, name="x_raw%d" % u) for u in range(2)]
+        dy_raw = [sb.tile([P, PACK, HALF], F32, name="dy_raw%d" % u) for u in range(2)]
+        x_packed = [sb.tile([P, HALF, PACK], BF16, name="x_packed%d" % u, align_bytes=64) for u in range(2)]
+        dy_packed = [sb.tile([P, HALF, PACK], BF16, name="dy_packed%d" % u, align_bytes=64) for u in range(2)]
         x_codes = sb.tile([P, N], U32, name="x_codes", align_bytes=64)
         dy_codes = sb.tile([P, N], U32, name="dy_codes", align_bytes=64)
         x_scales = sb.tile([P, N], U8, name="x_scales", align_bytes=64)
@@ -65,8 +64,6 @@ def tile_rows_bsoftmaxoftwo_kernel(
         s2 = sb.tile([P, M], U8, name="s2", align_bytes=64)
         so = sb.tile([P, M], U8, name="so", align_bytes=64)
         temper = sb.tile([P, G, HALVES], F32, name="temper")
-        warm_in = sb.tile([P, 1], F32, name="warm_in")
-        warm_out = sb.tile([P, 1], F32, name="warm_out")
         old_sb = [sb.tile([P, G, N], F32, name="old%d" % h) for h in range(HALVES)]
         z2_sb = [sb.tile([P, N], F32, name="z2_sb%d" % t) for t in range(4)]
         diff = [sb.tile([P, N], F32, name="diff%d" % t) for t in range(4)]
@@ -75,8 +72,8 @@ def tile_rows_bsoftmaxoftwo_kernel(
         result = [sb.tile([P, N], F32, name="result%d" % t) for t in range(4)]
         banks = [[psum.tile([P, N], F32, name="bank%d_%d" % (g, i)) for i in range(4)] for g in range(G)]
         z2_bank = [banks[g][2 * h] for g, h in TILES]
-        z1_bank = [banks[g][1 - h] for g, h in TILES]
-        c0_bank = [banks[g][3 - 2 * h] for g, h in TILES]
+        z1_bank = [banks[g][2 * h + 1] for g, h in TILES]
+        c0_bank = [banks[g][h] for g, h in TILES]
 
         def product(bank, words, wscales, codes, scales, t):
             g, h = TILES[t]
@@ -97,44 +94,66 @@ def tile_rows_bsoftmaxoftwo_kernel(
             )
 
         def copy_z2(t):
-            nc.scalar.copy(out=z2_sb[t][:], in_=z2_bank[t][:])
+            nc.scalar.activation(out=z2_sb[t][:], in_=z2_bank[t][:], func=ACT.Copy, scale=0.5)
 
-        def subtract(t):
-            nc.vector.tensor_tensor(out=diff[t][:], in0=z1_bank[t][:], in1=z2_sb[t][:], op=ALU.subtract)
+        def subtract(t, n0=0, n1=N):
+            nc.vector.scalar_tensor_tensor(
+                out=diff[t][:, n0:n1], in0=z1_bank[t][:, n0:n1], scalar=0.5, in1=z2_sb[t][:, n0:n1], op0=ALU.mult, op1=ALU.subtract
+            )
 
-        def sigmoid(t):
+        def sigmoid(t, n0=0, n1=N):
             g, h = TILES[t]
-            nc.scalar.activation(out=share[t][:], in_=diff[t][:], func=ACT.Sigmoid, scale=temper[:, g, h : h + 1])
+            nc.scalar.activation(out=share[t][:, n0:n1], in_=diff[t][:, n0:n1], func=ACT.Tanh, scale=temper[:, g, h : h + 1])
 
-        def multiply(t):
-            nc.vector.tensor_tensor(out=grad[t][:], in0=c0_bank[t][:], in1=share[t][:], op=ALU.mult)
+        def multiply(t, n0=0, n1=N):
+            nc.vector.scalar_tensor_tensor(
+                out=grad[t][:, n0:n1], in0=share[t][:, n0:n1], scalar=1.0, in1=c0_bank[t][:, n0:n1], op0=ALU.add, op1=ALU.mult
+            )
 
         def add_old(engine, t, n0=0, n1=N):
             g, h = TILES[t]
             engine.tensor_tensor(out=result[t][:, n0:n1], in0=grad[t][:, n0:n1], in1=old_sb[h][:, g, n0:n1], op=ALU.add)
 
-        def store(t, queue=nc.sync):
+        def store(t, queue=nc.sync, n0=0, n1=N):
             g, h = TILES[t]
-            queue.dma_start(out=out[g, P * h : P * (h + 1), :], in_=result[t][:])
+            queue.dma_start(out=out[g, P * h : P * (h + 1), n0:n1], in_=result[t][:, n0:n1])
 
-        for plane in (s2, s1, so):
+        for plane in (s1, s2, so):
             nc.vector.memset(plane[:].bitcast(I32), 0)
-        nc.vector.memset(warm_in[:], 0.0)
-        nc.scalar.activation(out=warm_out[:], in_=warm_in[:], func=ACT.Sigmoid)
 
+        x_rows = x.rearrange("g (p j) n -> (g p) j n", j=PACK)
+        dy_rows = dy.rearrange("g (p j) n -> (g p) j n", j=PACK)
         load_words(nc.sync, w2, w2_words)
         load_words(nc.sync, w1, w1_words)
-        nc.sync.dma_start(out=x_raw[:], in_=x.rearrange("g (p j) n -> (g p) j n", j=PACK))
+        for u in range(2):
+            nc.sync.dma_start(out=x_raw[u][:], in_=x_rows[:, :, HALF * u : HALF * (u + 1)])
         load_scales(nc.sync, s2, w2_scales)
-        load_scales(nc.sync, s1, w1_scales, (0, 1))
-        load_scales(nc.gpsimd, s1, w1_scales, (2, 3))
-        nc.sync.dma_start(out=dy_raw[:], in_=dy.rearrange("g (p j) n -> (g p) j n", j=PACK))
+        load_scales(nc.sync, s1, w1_scales, (0,))
+        load_scales(nc.gpsimd, s1, w1_scales, (1, 2, 3))
+        for u in range(2):
+            nc.sync.dma_start(out=dy_raw[u][:], in_=dy_rows[:, :, HALF * u : HALF * (u + 1)])
         with nc.allow_non_contiguous_dma(reason="one temper a partition"):
             nc.gpsimd.dma_start(out=temper[:], in_=tp.rearrange("g (h p) o -> p g (h o)", p=P))
         load_words(nc.sync, wo, wo_words)
         load_scales(nc.sync, so, wo_scales)
         for h in range(HALVES):
             nc.sync.dma_start(out=old_sb[h][:], in_=old[:, P * h : P * (h + 1), :].rearrange("g p n -> p g n"))
+
+        def pack(packed, raw, split, factor=1.0):
+            def vector_round(out, in_):
+                nc.vector.tensor_scalar(out=out, in0=in_, scalar1=factor, scalar2=None, op0=ALU.mult)
+
+            def scalar_round(out, in_):
+                nc.scalar.activation(out=out, in_=in_, func=ACT.Copy, scale=factor)
+
+            interleave(vector_round, packed, raw, 0, split)
+            interleave(scalar_round, packed, raw, split, raw.shape[2])
+
+        def quantize_half(codes, scales, packed, u):
+            cols = slice(HALF * u, HALF * (u + 1))
+            nc.vector.quantize_mx(
+                out=codes[:, cols].bitcast(FP8X4), scales=scales[:, cols], in_=packed[u][:].rearrange("p n j -> p (n j)")
+            )
 
         def z1_product(t):
             product(z1_bank[t], w1, s1, x_codes, x_scales, t)
@@ -145,44 +164,47 @@ def tile_rows_bsoftmaxoftwo_kernel(
         def c0_product(t):
             product(c0_bank[t], wo, so, dy_codes, dy_scales, t)
 
-        interleave(nc.vector.tensor_copy, x_packed, x_raw, 0, X_SPLIT)
-        interleave(nc.scalar.copy, x_packed, x_raw, X_SPLIT, N)
-        quantize(x_codes, x_scales, x_packed)
+        pack(x_packed[0], x_raw[0], 168)
+        quantize_half(x_codes, x_scales, x_packed, 0)
+        pack(x_packed[1], x_raw[1], 168)
+        quantize_half(x_codes, x_scales, x_packed, 1)
         z2_product(0)
         z2_product(1)
         z1_product(0)
         z1_product(1)
         z2_product(2)
         z2_product(3)
-
-        copy_z2(0)
-        interleave(nc.vector.tensor_copy, dy_packed, dy_raw, 0, DY_SPLIT)
-        interleave(nc.scalar.copy, dy_packed, dy_raw, DY_SPLIT, N)
-        copy_z2(1)
-        subtract(0)
-        quantize(dy_codes, dy_scales, dy_packed)
-        subtract(1)
-        c0_product(0)
-        c0_product(1)
         z1_product(2)
         z1_product(3)
-        c0_product(2)
-        c0_product(3)
-        sigmoid(0)
+        pack(dy_packed[0], dy_raw[0], 168, 0.5)
+        copy_z2(0)
+        quantize_half(dy_codes, dy_scales, dy_packed, 0)
+        pack(dy_packed[1], dy_raw[1], 168, 0.5)
+        copy_z2(1)
+        subtract(0)
+        quantize_half(dy_codes, dy_scales, dy_packed, 1)
+        subtract(1)
         copy_z2(2)
+        subtract(2)
+        for t in range(4):
+            c0_product(t)
+        sigmoid(0)
         sigmoid(1)
         copy_z2(3)
         for t in (0, 1):
             multiply(t)
             add_old(nc.gpsimd, t)
             store(t)
-        for t in (2, 3):
-            subtract(t)
-            sigmoid(t)
+        sigmoid(2)
+        for n0 in (0, HALF):
+            subtract(3, n0, n0 + HALF)
+            sigmoid(3, n0, n0 + HALF)
         multiply(2)
-        add_old(nc.gpsimd, 2, 0, N // 2)
-        multiply(3)
-        add_old(nc.vector, 2, N // 2, N)
+        multiply(3, 0, HALF)
+        multiply(3, HALF, N)
+        add_old(nc.vector, 2)
         store(2)
-        add_old(nc.vector, 3)
-        store(3, nc.scalar)
+        add_old(nc.vector, 3, 0, HALF)
+        store(3, nc.scalar, 0, HALF)
+        add_old(nc.vector, 3, HALF, N)
+        store(3, nc.sync, HALF, N)

@@ -128,14 +128,14 @@ def tile_rows_bsoftmaxoftwo_kernel(
         for u in range(2):
             nc.sync.dma_start(out=x_raw[u][:], in_=x_rows[:, :, HALF * u : HALF * (u + 1)])
         load_scales(nc.sync, s2, w2_scales)
-        load_scales(nc.sync, s1, w1_scales, (0,))
-        load_scales(nc.gpsimd, s1, w1_scales, (1, 2, 3))
+        load_scales(nc.sync, s1, w1_scales, (0, 1))
+        load_scales(nc.gpsimd, s1, w1_scales, (2, 3))
         for u in range(2):
             nc.sync.dma_start(out=dy_raw[u][:], in_=dy_rows[:, :, HALF * u : HALF * (u + 1)])
-        with nc.allow_non_contiguous_dma(reason="one temper a partition"):
-            nc.gpsimd.dma_start(out=temper[:], in_=tp.rearrange("g (h p) o -> p g (h o)", p=P))
         load_words(nc.sync, wo, wo_words)
         load_scales(nc.sync, so, wo_scales)
+        with nc.allow_non_contiguous_dma(reason="one temper a partition"):
+            nc.sync.dma_start(out=temper[:], in_=tp.rearrange("g (h p) o -> p g (h o)", p=P))
         for h in range(HALVES):
             nc.sync.dma_start(out=old_sb[h][:], in_=old[:, P * h : P * (h + 1), :].rearrange("g p n -> p g n"))
 
@@ -191,10 +191,12 @@ def tile_rows_bsoftmaxoftwo_kernel(
         sigmoid(0)
         sigmoid(1)
         copy_z2(3)
-        for t in (0, 1):
-            multiply(t)
-            add_old(nc.gpsimd, t)
-            store(t)
+        for n0 in (0, HALF):
+            multiply(0, n0, n0 + HALF)
+            add_old(nc.gpsimd, 0, n0, n0 + HALF)
+        store(0)
+        multiply(1)
+        add_old(nc.gpsimd, 1, 0, HALF)
         sigmoid(2)
         for n0 in (0, HALF):
             subtract(3, n0, n0 + HALF)
@@ -202,6 +204,8 @@ def tile_rows_bsoftmaxoftwo_kernel(
         multiply(2)
         multiply(3, 0, HALF)
         multiply(3, HALF, N)
+        add_old(nc.vector, 1, HALF, N)
+        store(1)
         add_old(nc.vector, 2)
         store(2)
         add_old(nc.vector, 3, 0, HALF)

@@ -128,8 +128,8 @@ def tile_rows_bsoftmaxoftwo_kernel(
         for u in range(2):
             nc.sync.dma_start(out=x_raw[u][:], in_=x_rows[:, :, HALF * u : HALF * (u + 1)])
         load_scales(nc.sync, s2, w2_scales)
-        load_scales(nc.sync, s1, w1_scales, (0, 1))
-        load_scales(nc.gpsimd, s1, w1_scales, (2, 3))
+        load_scales(nc.sync, s1, w1_scales, (0,))
+        load_scales(nc.gpsimd, s1, w1_scales, (1, 2, 3))
         for u in range(2):
             nc.sync.dma_start(out=dy_raw[u][:], in_=dy_rows[:, :, HALF * u : HALF * (u + 1)])
         load_words(nc.sync, wo, wo_words)
@@ -164,9 +164,9 @@ def tile_rows_bsoftmaxoftwo_kernel(
         def c0_product(t):
             product(c0_bank[t], wo, so, dy_codes, dy_scales, t)
 
-        pack(x_packed[0], x_raw[0], 168)
+        pack(x_packed[0], x_raw[0], 176)
         quantize_half(x_codes, x_scales, x_packed, 0)
-        pack(x_packed[1], x_raw[1], 168)
+        pack(x_packed[1], x_raw[1], 176)
         quantize_half(x_codes, x_scales, x_packed, 1)
         z2_product(0)
         z2_product(1)
@@ -176,10 +176,10 @@ def tile_rows_bsoftmaxoftwo_kernel(
         z2_product(3)
         z1_product(2)
         z1_product(3)
-        pack(dy_packed[0], dy_raw[0], 168, 0.5)
+        pack(dy_packed[0], dy_raw[0], 176, 0.5)
         copy_z2(0)
         quantize_half(dy_codes, dy_scales, dy_packed, 0)
-        pack(dy_packed[1], dy_raw[1], 168, 0.5)
+        pack(dy_packed[1], dy_raw[1], 176, 0.5)
         copy_z2(1)
         subtract(0)
         quantize_half(dy_codes, dy_scales, dy_packed, 1)

from contextlib import ExitStack

import concourse.mybir as mybir

G, D, M, N = 2, 256, 256, 512
FLOPS = 3 * 2 * G * D * M * N

F32 = mybir.dt.float32
BF16 = mybir.dt.bfloat16
I32 = mybir.dt.int32
U32 = mybir.dt.uint32
U8 = mybir.dt.uint8
FP8X4 = mybir.dt.float8_e4m3fn_x4
FP4X4 = mybir.dt.float4_e2m1fn_x4
ALU = mybir.AluOpType
ACT = mybir.ActivationFunctionType

P = 128
PACK = 4
ROWS = D // PACK
HALVES = M // P
TILES = [(g, h) for h in range(HALVES) for g in range(G)]
HALF = N // 2


def load_words(queue, tile, words):
    queue.dma_start(out=tile[:].bitcast(I32), in_=words.rearrange("g p b -> (g p) b").bitcast(I32))


def load_scales(queue, tile, scales, quadrants=(0, 1, 2, 3)):
    rows = scales.rearrange("g t m -> (g t) m").bitcast(I32)
    for q in quadrants:
        queue.dma_start(out=tile[32 * q : 32 * q + 4, :].bitcast(I32), in_=rows[4 * q : 4 * q + 4, :])


def interleave(copy, packed, raw, n0, n1):
    copy(
        out=packed[:, n0:n1, :].rearrange("p (c i) j -> p c j i", i=4),
        in_=raw[:, :, n0:n1].rearrange("p j (c i) -> p c j i", i=4),
    )


def tile_rows_bsoftmaxoftwo_kernel(
    tc, x, w1_words, w1_scales, w2_words, w2_scales, tp, wo_words, wo_scales, dy, old, out
):
    nc = tc.nc
    with ExitStack() as ctx:
        sb = ctx.enter_context(tc.tile_pool(name="sb", bufs=1))
        psum = ctx.enter_context(tc.psum_pool(name="psum", bufs=1))
        ctx.enter_context(tc.manual_schedule())

        x_raw = [sb.tile([P, PACK, HALF], F32, name="x_raw%d" % u) for u in range(2)]
        dy_raw = [sb.tile([P, PACK, HALF], F32, name="dy_raw%d" % u) for u in range(2)]
        x_packed = [sb.tile([P, HALF, PACK], BF16, name="x_packed%d" % u, align_bytes=64) for u in range(2)]
        dy_packed = [sb.tile([P, HALF, PACK], BF16, name="dy_packed%d" % u, align_bytes=64) for u in range(2)]
        x_codes = sb.tile([P, N], U32, name="x_codes", align_bytes=64)
        dy_codes = sb.tile([P, N], U32, name="dy_codes", align_bytes=64)
        x_scales = sb.tile([P, N], U8, name="x_scales", align_bytes=64)
        dy_scales = sb.tile([P, N], U8, name="dy_scales", align_bytes=64)
        w1 = sb.tile([P, 2 * M], U8, name="w1", align_bytes=64)
        w2 = sb.tile([P, 2 * M], U8, name="w2", align_bytes=64)
        wo = sb.tile([P, 2 * M], U8, name="wo", align_bytes=64)
        s1 = sb.tile([P, M], U8, name="s1", align_bytes=64)
        s2 = sb.tile([P, M], U8, name="s2", align_bytes=64)
        so = sb.tile([P, M], U8, name="so", align_bytes=64)
        temper = sb.tile([P, G, HALVES], F32, name="temper")
        old_sb = [sb.tile([P, G, N], F32, name="old%d" % h) for h in range(HALVES)]
        z2_sb = [sb.tile([P, N], F32, name="z2_sb%d" % t) for t in range(4)]
        diff = [sb.tile([P, N], F32, name="diff%d" % t) for t in range(4)]
        share = [sb.tile([P, N], F32, name="share%d" % t) for t in range(4)]
        grad = [sb.tile([P, N], F32, name="grad%d" % t) for t in range(4)]
        result = [sb.tile([P, N], F32, name="result%d" % t) for t in range(4)]
        banks = [[psum.tile([P, N], F32, name="bank%d_%d" % (g, i)) for i in range(4)] for g in range(G)]
        z2_bank = [banks[g][2 * h] for g, h in TILES]
        z1_bank = [banks[g][2 * h + 1] for g, h in TILES]
        c0_bank = [banks[g][h] for g, h in TILES]

        def product(bank, words, wscales, codes, scales, t):
            g, h = TILES[t]
            rows = slice(ROWS * g, ROWS * (g + 1))
            nc.tensor.matmul_mx(
                out=bank[:],
                lhsT=words[rows, 2 * P * h : 2 * P * (h + 1)].bitcast(FP4X4),
                lhsT_scale=wscales[rows, P * h : P * (h + 1)],
                rhs=codes[rows, :].bitcast(FP8X4),
                rhs_scale=scales[rows, :],
                start=True,
                stop=True,
            )

        def quantize(codes, scales, packed):
            nc.vector.quantize_mx(
                out=codes[:].bitcast(FP8X4), scales=scales[:], in_=packed[:].rearrange("p n j -> p (n j)")
            )

        def copy_z2(t):
            nc.scalar.activation(out=z2_sb[t][:], in_=z2_bank[t][:], func=ACT.Copy, scale=0.5)

        def subtract(t, n0=0, n1=N):
            nc.vector.scalar_tensor_tensor(
                out=diff[t][:, n0:n1], in0=z1_bank[t][:, n0:n1], scalar=0.5, in1=z2_sb[t][:, n0:n1], op0=ALU.mult, op1=ALU.subtract
            )

        def sigmoid(t, n0=0, n1=N):
            g, h = TILES[t]
            nc.scalar.activation(out=share[t][:, n0:n1], in_=diff[t][:, n0:n1], func=ACT.Tanh, scale=temper[:, g, h : h + 1])

        def multiply(t, n0=0, n1=N):
            nc.vector.scalar_tensor_tensor(
                out=grad[t][:, n0:n1], in0=share[t][:, n0:n1], scalar=1.0, in1=c0_bank[t][:, n0:n1], op0=ALU.add, op1=ALU.mult
            )

        def add_old(engine, t, n0=0, n1=N):
            g, h = TILES[t]
            engine.tensor_tensor(out=result[t][:, n0:n1], in0=grad[t][:, n0:n1], in1=old_sb[h][:, g, n0:n1], op=ALU.add)

        def store(t, queue=nc.sync, n0=0, n1=N):
            g, h = TILES[t]
            queue.dma_start(out=out[g, P * h : P * (h + 1), n0:n1], in_=result[t][:, n0:n1])

        for plane in (s1, s2, so):
            nc.vector.memset(plane[:].bitcast(I32), 0)

        x_rows = x.rearrange("g (p j) n -> (g p) j n", j=PACK)
        dy_rows = dy.rearrange("g (p j) n -> (g p) j n", j=PACK)
        load_words(nc.sync, w2, w2_words)
        load_words(nc.sync, w1, w1_words)
        for u in range(2):
            nc.sync.dma_start(out=x_raw[u][:], in_=x_rows[:, :, HALF * u : HALF * (u + 1)])
        load_scales(nc.sync, s2, w2_scales)
        load_scales(nc.sync, s1, w1_scales, (0,))
        load_scales(nc.gpsimd, s1, w1_scales, (1, 2, 3))
        for u in range(2):
            nc.sync.dma_start(out=dy_raw[u][:], in_=dy_rows[:, :, HALF * u : HALF * (u + 1)])
        load_words(nc.sync, wo, wo_words)
        load_scales(nc.sync, so, wo_scales)
        with nc.allow_non_contiguous_dma(reason="one temper a partition"):
            nc.sync.dma_start(out=temper[:], in_=tp.rearrange("g (h p) o -> p g (h o)", p=P))
        for h in range(HALVES):
            nc.sync.dma_start(out=old_sb[h][:], in_=old[:, P * h : P * (h + 1), :].rearrange("g p n -> p g n"))

        def pack(packed, raw, split, factor=1.0):
            def vector_round(out, in_):
                nc.vector.tensor_scalar(out=out, in0=in_, scalar1=factor, scalar2=None, op0=ALU.mult)

            def scalar_round(out, in_):
                nc.scalar.activation(out=out, in_=in_, func=ACT.Copy, scale=factor)

            interleave(vector_round, packed, raw, 0, split)
            interleave(scalar_round, packed, raw, split, raw.shape[2])

        def quantize_half(codes, scales, packed, u):
            cols = slice(HALF * u, HALF * (u + 1))
            nc.vector.quantize_mx(
                out=codes[:, cols].bitcast(FP8X4), scales=scales[:, cols], in_=packed[u][:].rearrange("p n j -> p (n j)")
            )

        def z1_product(t):
            product(z1_bank[t], w1, s1, x_codes, x_scales, t)

        def z2_product(t):
            product(z2_bank[t], w2, s2, x_codes, x_scales, t)

        def c0_product(t):
            product(c0_bank[t], wo, so, dy_codes, dy_scales, t)

        pack(x_packed[0], x_raw[0], 176)
        quantize_half(x_codes, x_scales, x_packed, 0)
        pack(x_packed[1], x_raw[1], 176)
        quantize_half(x_codes, x_scales, x_packed, 1)
        z2_product(0)
        z2_product(1)
        z1_product(0)
        z1_product(1)
        z2_product(2)
        z2_product(3)
        z1_product(2)
        z1_product(3)
        pack(dy_packed[0], dy_raw[0], 176, 0.5)
        copy_z2(0)
        quantize_half(dy_codes, dy_scales, dy_packed, 0)
        pack(dy_packed[1], dy_raw[1], 176, 0.5)
        copy_z2(1)
        subtract(0)
        quantize_half(dy_codes, dy_scales, dy_packed, 1)
        subtract(1)
        copy_z2(2)
        subtract(2)
        for t in range(4):
            c0_product(t)
        sigmoid(0)
        sigmoid(1)
        copy_z2(3)
        for n0 in (0, HALF):
            multiply(0, n0, n0 + HALF)
            add_old(nc.gpsimd, 0, n0, n0 + HALF)
        store(0)
        multiply(1)
        add_old(nc.gpsimd, 1, 0, HALF)
        sigmoid(2)
        for n0 in (0, HALF):
            subtract(3, n0, n0 + HALF)
            sigmoid(3, n0, n0 + HALF)
        multiply(2)
        multiply(3, 0, HALF)
        multiply(3, HALF, N)
        add_old(nc.vector, 1, HALF, N)
        store(1)
        add_old(nc.vector, 2)
        store(2)
        add_old(nc.vector, 3, 0, HALF)
        store(3, nc.scalar, 0, HALF)
        add_old(nc.vector, 3, HALF, N)
        store(3, nc.sync, HALF, N)
